import numpy as np
import ml_dtypes


def mxq(x, axis, fmt="e4m3"):
    dtype, down = {"e4m3": (ml_dtypes.float8_e4m3fn, 7), "e5m2": (ml_dtypes.float8_e5m2, 14)}[fmt]
    v = np.moveaxis(np.asarray(x, np.float32).astype(ml_dtypes.bfloat16).astype(np.float64), axis, -1)
    blocks = v.reshape(v.shape[:-1] + (-1, 32))
    amax = np.abs(blocks).max(-1, keepdims=True)
    byte = np.maximum(np.where(amax > 0, np.frexp(amax)[1] - 1 + 127, 0) - down, 1)
    scale = np.exp2(byte - 127.0)
    codes = (blocks / scale).astype(np.float32).astype(dtype).astype(np.float64)
    return np.moveaxis((codes * scale).reshape(v.shape), -1, axis)


WIDE = False


def mx_kscale(k):
    if not WIDE:
        return np.ones(k)
    levels = np.array([10, -10, 5, -5, 0])
    if k % 512:
        return np.exp2(np.random.permutation(np.resize(levels, k // 32))).repeat(32)
    a = np.empty((k // 512, 16))
    for p in range(k // 512):
        a[p, :8] = np.random.permutation(np.resize(levels, 8))
        for g in range(8):
            far = levels[np.abs(levels - a[p, g]) >= 10]
            a[p, g + 8] = far[np.random.randint(len(far))]
    return np.exp2(a.ravel()).repeat(32)


def f64(x):
    return np.asarray(x).astype(np.float64)


def striped(idx):
    return np.tile(idx.reshape(-1, 16).T, (8, 1)).astype(np.uint16)


def unstriped(offs):
    return offs[:16].T.reshape(-1).astype(np.int64)


def pack_weight(w):
    k, n = w.shape
    w = f64(np.asarray(w, np.float32).astype(ml_dtypes.bfloat16)).reshape(k // 32, 32, n)
    amax = np.abs(w).max(1)
    byte = np.clip(np.where(amax > 0, np.frexp(amax)[1] - 1 + 127 - 7, 1), 1, 254)
    scaled = (w * np.exp2(127.0 - byte)[:, None, :]).reshape(k, n).astype(np.float32)
    words = np.ascontiguousarray(scaled.reshape(k // 512, 128, 4, n).transpose(0, 1, 3, 2)).astype(ml_dtypes.float8_e4m3fn).view(np.uint8)
    return words, np.ascontiguousarray(byte.astype(np.uint8).reshape(k // 512, 16, n))


def unpack_weight(words, scales):
    g, p, n, _ = words.shape
    vals = np.ascontiguousarray(words).view(ml_dtypes.float8_e4m3fn).astype(np.float64) * np.repeat(np.exp2(scales.astype(np.float64) - 127.0), 8, axis=1)[..., None]
    return vals.transpose(0, 1, 3, 2).reshape(g * 512, n)

def planes(y):
    n, m = y.shape
    v = y.astype(np.float32).astype(ml_dtypes.bfloat16).astype(np.float64).reshape(n // 32, 32, m)
    top = np.abs(v).max(1)
    byte = np.clip(np.where(top > 0, np.frexp(top)[1] - 1 + 127 - 7, 1), 1, 254)
    codes = (v * np.exp2(127.0 - byte)[:, None, :]).reshape(n, m).astype(np.float32).astype(ml_dtypes.float8_e4m3fn).view(np.uint8)
    words = codes.reshape(n // 512, 128, 4, m).transpose(0, 1, 3, 2)
    return np.ascontiguousarray(words), np.ascontiguousarray(byte.astype(np.uint8).reshape(n // 512, 16, m))


K, T, H = 512, 512, 512


def setup_inputs():
    n = np.random.standard_normal
    s = mx_kscale(K)[:, None]
    u = mx_kscale(H)
    packed_xT = pack_weight(n((K, T)) * s)
    return {
        "x_words": packed_xT[0],
        "x_scales": packed_xT[1],
        "w1": (n((K, H)) / np.sqrt(K) / s * u).astype(np.float32),
        "w2": (n((H, H)) / np.sqrt(3 * H) / u[:, None]).astype(np.float32),
        "w3": (n((H, H)) / np.sqrt(3 * H) / u[:, None]).astype(np.float32),
        "w4": (n((H, H)) / np.sqrt(3 * H) / u[:, None]).astype(np.float32),
        "pos1": striped(np.random.permutation(T)),
        "pos2": striped(np.random.permutation(T)),
        "pos3": striped(np.random.permutation(T)),
        "pos4": striped(np.random.permutation(T)),
    }


def reference(x_words, x_scales, w1, w2, w3, w4, pos1, pos2, pos3, pos4):
    xq = unpack_weight(x_words, x_scales)
    h = mxq(f64(w1), 0, "e4m3").T @ xq
    g0 = h[:, unstriped(pos1)]
    g1 = h[:, unstriped(pos2)]
    g2 = h[:, unstriped(pos3)]
    g3 = h[:, unstriped(pos4)]
    z1 = (g0 + g1 + g2 + g3) / 4
    z2 = np.maximum(np.maximum(np.maximum(g0, g1), g2), g3)
    z3 = np.minimum(np.minimum(np.minimum(g0, g1), g2), g3)
    out_0 = mxq(f64(w2), 0, "e4m3").T @ mxq(z1, 0, "e4m3") + mxq(f64(w3), 0, "e4m3").T @ mxq(z2, 0, "e4m3") + mxq(f64(w4), 0, "e4m3").T @ mxq(z3, 0, "e4m3")
    return (out_0,) + planes(out_0)

@@ -1,0 +1,194 @@
+from contextlib import ExitStack
+
+import concourse.mybir as mybir
+from concourse.masks import make_identity
+
+FLOPS = 4 * 2 * 512 * 512 * 512
+
+F32 = mybir.dt.float32
+BF16 = mybir.dt.bfloat16
+U32 = mybir.dt.uint32
+I32 = mybir.dt.int32
+U16 = mybir.dt.uint16
+U8 = mybir.dt.uint8
+FP8X4 = mybir.dt.float8_e4m3fn_x4
+MAX = mybir.AluOpType.max
+MIN = mybir.AluOpType.min
+COPY = mybir.ActivationFunctionType.Copy
+
+P = 128
+PACK = 4
+T = 512
+D = 4
+CHUNK = 256
+BLOCK = 128
+
+
+def tile_picked_wpna_none_lo_kernel(
+    tc, x_words, x_scales, w1, w2, w3, w4, pos1, pos2, pos3, pos4, out_0, out_1, out_2
+):
+    nc = tc.nc
+    with ExitStack() as ctx:
+        sb = ctx.enter_context(tc.tile_pool(name="sb", bufs=1))
+        ps = ctx.enter_context(tc.psum_pool(name="ps", bufs=1))
+
+        def bank(b, shape, name):
+            return ps.tile(shape, F32, name=name, tag=f"bank{b}")
+
+        lists = [sb.tile([P, T // 16], U16, name=f"list{d}") for d in range(D)]
+        x_codes = sb.tile([P, T], U32, align_bytes=64)
+        x_plane = sb.tile([P, T], U8, align_bytes=64)
+        ident = sb.tile([P, P], F32)
+        w1_raw = [sb.tile([P, PACK, T // 2], F32, name=f"w1_raw{a}") for a in range(2)]
+        w_raw = [sb.tile([P, PACK, T], F32, name=f"w_raw{k}") for k in range(3)]
+
+        nc.vector.memset(x_plane[:].bitcast(U32), 0)
+        for q in range(4):
+            nc.scalar.dma_start(out=x_plane[32 * q : 32 * q + 4, :].bitcast(I32), in_=x_scales[0, 4 * q : 4 * q + 4, :].bitcast(I32))
+        w1_rows = w1.rearrange("(p j) c -> p j c", j=PACK)
+        for a in range(2):
+            nc.sync.dma_start(out=w1_raw[a][:], in_=w1_rows[:, :, a * 256 : (a + 1) * 256])
+        nc.sync.dma_start(out=x_codes[:].bitcast(I32), in_=x_words[0].rearrange("p n t -> p (n t)").bitcast(I32))
+        later = [(w_raw[k], w.rearrange("(p j) c -> p j c", j=PACK)) for k, w in enumerate((w2, w3, w4))]
+        for d, pos in enumerate((pos1, pos2, pos3, pos4)):
+            nc.sync.dma_start(lists[d][:], pos)
+        for raw, rows in later:
+            nc.sync.dma_start(out=raw[:], in_=rows)
+        make_identity(nc, ident[:])
+
+        def dealt(tile):
+            return tile[:].rearrange("p (t m j) -> p m t j", t=PACK, j=PACK)
+
+        def by_column(raw):
+            return raw[:].rearrange("p j (m t) -> p m t j", t=PACK)
+
+        w1_b = sb.tile([P, PACK * T], BF16, align_bytes=64)
+        w1_codes = sb.tile([P, T], U32, align_bytes=64)
+        w1_plane = sb.tile([P, T], U8, align_bytes=64)
+        for a in range(2):
+            nc.vector.tensor_copy(out=dealt(w1_b)[:, a * 64 : (a + 1) * 64], in_=by_column(w1_raw[a]))
+        h = []
+        for t in range(PACK):
+            cols = slice(t * P, (t + 1) * P)
+            nc.vector.quantize_mx(out=w1_codes[:, cols].bitcast(FP8X4), scales=w1_plane[:, cols], in_=w1_b[:, t * T : (t + 1) * T])
+            acc = bank(t, [P, T], f"h_acc{t}")
+            nc.tensor.matmul_mx(out=acc[:], lhsT=w1_codes[:, cols].bitcast(FP8X4), lhsT_scale=w1_plane[:, cols],
+                                rhs=x_codes[:].bitcast(FP8X4), rhs_scale=x_plane[:], start=True, stop=True)
+            h_t = sb.tile([P, T], F32, name=f"h{t}")
+            nc.scalar.copy(out=h_t[:], in_=acc[:])
+            h.append(h_t)
+
+        g = {}
+        for c in range(2):
+            for d in range(D):
+                g[c, d] = sb.tile([P, PACK, CHUNK], F32, name=f"g{c}{d}")
+                for t in range(PACK):
+                    nc.vector.tensor_copy(g[c, d][:, t, :], h[t][:].indirect(lists[d][:, c * 16 : (c + 1) * 16]))
+
+        w_b = [sb.tile([P, PACK * T], BF16, name=f"w_b{k}", align_bytes=64) for k in range(3)]
+        w_codes = [sb.tile([P, T], U32, name=f"w_codes{k}", align_bytes=64) for k in range(3)]
+        w_plane = [sb.tile([P, T], U8, name=f"w_plane{k}", align_bytes=64) for k in range(3)]
+        g_b = [sb.tile([P, D, CHUNK * PACK], BF16, name=f"g_b{c}", align_bytes=64) for c in range(2)]
+        z_b = [[sb.tile([P, CHUNK * PACK], BF16, name=f"z_b{c}{k}", align_bytes=64) for k in range(3)] for c in range(2)]
+        z_codes = [sb.tile([P, T], U32, name=f"z_codes{k}", align_bytes=64) for k in range(3)]
+        z_plane = [sb.tile([P, T], U8, name=f"z_plane{k}", align_bytes=64) for k in range(3)]
+
+        def round_weight(k):
+            nc.scalar.copy(out=dealt(w_b[k]), in_=by_column(w_raw[k]))
+
+        def round_gathered(c, d):
+            nc.scalar.copy(out=g_b[c][:, d, :].rearrange("p (n i t) -> p n t i", t=PACK, i=4),
+                           in_=g[c, d][:].rearrange("p t (n i) -> p n t i", i=4))
+
+        def sum_turned(c):
+            sums = [bank(4 + 2 * c + b, [P, PACK, P], f"sum{c}{b}") for b in range(2)]
+            for d in range(D):
+                for t in range(PACK):
+                    for b in range(2):
+                        nc.tensor.matmul(sums[b][:, t, :], g[c, d][:, t, b * BLOCK : (b + 1) * BLOCK], ident[:], is_transpose=True,
+                                         start=(d == 0 and t == 0), stop=(d == D - 1 and t == PACK - 1))
+            return sums
+
+        def mean_back(c, sums):
+            back = bank(c, [P, 2, 2, BLOCK], f"back{c}")
+            for b in range(2):
+                mean_t = sb.tile([P, 2 * P * 2], BF16, name=f"mean_t{c}{b}")
+                nc.scalar.activation(mean_t[:].rearrange("v (u p e) -> v u p e", u=2, e=2),
+                                     sums[b][:].rearrange("v (u e) p -> v u p e", e=2), COPY, scale=0.25)
+                words = mean_t[:].bitcast(F32)
+                for u in range(2):
+                    nc.tensor.transpose(back[:, b, u, :], words[:, u * P : (u + 1) * P], ident[:])
+            nc.scalar.copy(out=z_b[c][0][:].bitcast(F32).rearrange("p (b v u) -> p b v u", b=2, u=2),
+                           in_=back[:].rearrange("p b u v -> p b v u"))
+
+        sums0 = sum_turned(0)
+        sums1 = sum_turned(1)
+        round_weight(0)
+        round_gathered(0, 0)
+        round_gathered(0, 1)
+        round_weight(1)
+        round_gathered(0, 2)
+        round_gathered(0, 3)
+        mean_back(0, sums0)
+        round_weight(2)
+        for d in range(D):
+            round_gathered(1, d)
+        mean_back(1, sums1)
+
+        def first_level(c):
+            pair = []
+            for op, name in ((MAX, "hi"), (MIN, "lo")):
+                two = sb.tile([P, 2, CHUNK * PACK], BF16, name=f"{name}{c}", align_bytes=64)
+                nc.vector.tensor_tensor(two[:], g_b[c][:, 0:2, :], g_b[c][:, 2:4, :], op)
+                pair.append(two)
+            return pair
+
+        def statistics(c, pair, v0, n):
+            span = slice((v0 - c * CHUNK) * PACK, (v0 - c * CHUNK + n) * PACK)
+            for k, op in ((1, MAX), (2, MIN)):
+                nc.vector.tensor_tensor(z_b[c][k][:, span], pair[k - 1][:, 0, span], pair[k - 1][:, 1, span], op)
+            for k in range(3):
+                nc.vector.quantize_mx(out=z_codes[k][:, v0 : v0 + n].bitcast(FP8X4), scales=z_plane[k][:, v0 : v0 + n], in_=z_b[c][k][:, span])
+
+        y = sb.tile([P, PACK, T], F32)
+        y_b = sb.tile([P, T * PACK], BF16, align_bytes=64)
+        y_codes = sb.tile([P, T], U32, align_bytes=64)
+        y_plane = sb.tile([P, T], U8, align_bytes=64)
+        out_rows = out_0.rearrange("(p t) v -> p t v", t=PACK)
+        out_words = out_1[0].rearrange("p n t -> p (n t)").bitcast(I32)
+
+        def product(j):
+            cols = slice(j * BLOCK, (j + 1) * BLOCK)
+            acc = bank((2, 3, 4, 5)[j], [P, PACK, BLOCK], f"y_acc{j}")
+            for t in range(PACK):
+                m = slice(t * P, (t + 1) * P)
+                for k in range(3):
+                    nc.tensor.matmul_mx(out=acc[:, t, :], lhsT=w_codes[k][:, m].bitcast(FP8X4), lhsT_scale=w_plane[k][:, m],
+                                        rhs=z_codes[k][:, cols].bitcast(FP8X4), rhs_scale=z_plane[k][:, cols],
+                                        start=(k == 0), stop=(k == 2))
+            nc.scalar.copy(out=y_b[:, j * BLOCK * PACK : (j + 1) * BLOCK * PACK].rearrange("p (v t) -> p v t", t=PACK),
+                           in_=acc[:].rearrange("p t v -> p v t"))
+            nc.scalar.copy(out=y[:, :, cols], in_=acc[:])
+
+        def hand_out(v0, n):
+            cols = slice(v0, v0 + n)
+            nc.sync.dma_start(out=out_rows[:, :, cols], in_=y[:, :, cols])
+            nc.vector.quantize_mx(out=y_codes[:, cols].bitcast(FP8X4), scales=y_plane[:, cols], in_=y_b[:, v0 * PACK : (v0 + n) * PACK])
+            nc.sync.dma_start(out=out_words[:, cols], in_=y_codes[:, cols].bitcast(I32))
+
+        pair0 = first_level(0)
+        for k in range(3):
+            nc.vector.quantize_mx(out=w_codes[k][:].bitcast(FP8X4), scales=w_plane[k][:], in_=w_b[k][:])
+        statistics(0, pair0, 0, CHUNK)
+        product(0)
+        product(1)
+        pair1 = first_level(1)
+        statistics(1, pair1, 256, BLOCK)
+        product(2)
+        hand_out(0, CHUNK)
+        statistics(1, pair1, 384, BLOCK)
+        product(3)
+        hand_out(256, BLOCK)
+        hand_out(384, BLOCK)
+        for q in range(4):
+            nc.sync.dma_start(out=out_2[0, 4 * q : 4 * q + 4, :].bitcast(I32), in_=y_plane[32 * q : 32 * q + 4, :].bitcast(I32))

@@ -20,8 +20,10 @@ P = 128
 PACK = 4
 T = 512
 D = 4
-CHUNK = 256
+HALF = 256
 BLOCK = 128
+WINDOW = 704
+VECTOR_M = 40
 
 
 def tile_picked_wpna_none_lo_kernel(
@@ -39,25 +41,27 @@ def tile_picked_wpna_none_lo_kernel(
         x_codes = sb.tile([P, T], U32, align_bytes=64)
         x_plane = sb.tile([P, T], U8, align_bytes=64)
         ident = sb.tile([P, P], F32)
-        w1_raw = [sb.tile([P, PACK, T // 2], F32, name=f"w1_raw{a}") for a in range(2)]
+        w1_raw = [sb.tile([P, PACK, HALF], F32, name=f"w1_raw{a}") for a in range(2)]
         w_raw = [sb.tile([P, PACK, T], F32, name=f"w_raw{k}") for k in range(3)]
+        h = [sb.tile([P, WINDOW], F32, name=f"h{t}") for t in range(PACK)]
 
         nc.vector.memset(x_plane[:].bitcast(U32), 0)
         for q in range(4):
             nc.scalar.dma_start(out=x_plane[32 * q : 32 * q + 4, :].bitcast(I32), in_=x_scales[0, 4 * q : 4 * q + 4, :].bitcast(I32))
         w1_rows = w1.rearrange("(p j) c -> p j c", j=PACK)
         for a in range(2):
-            nc.sync.dma_start(out=w1_raw[a][:], in_=w1_rows[:, :, a * 256 : (a + 1) * 256])
+            nc.sync.dma_start(out=w1_raw[a][:], in_=w1_rows[:, :, a * HALF : (a + 1) * HALF])
         nc.sync.dma_start(out=x_codes[:].bitcast(I32), in_=x_words[0].rearrange("p n t -> p (n t)").bitcast(I32))
-        later = [(w_raw[k], w.rearrange("(p j) c -> p j c", j=PACK)) for k, w in enumerate((w2, w3, w4))]
         for d, pos in enumerate((pos1, pos2, pos3, pos4)):
             nc.sync.dma_start(lists[d][:], pos)
-        for raw, rows in later:
-            nc.sync.dma_start(out=raw[:], in_=rows)
+        for k, w in enumerate((w2, w3, w4)):
+            nc.sync.dma_start(out=w_raw[k][:], in_=w.rearrange("(p j) c -> p j c", j=PACK))
+        for t in range(PACK):
+            nc.gpsimd.memset(h[t][:, T:], 0.0)
         make_identity(nc, ident[:])
 
-        def dealt(tile):
-            return tile[:].rearrange("p (t m j) -> p m t j", t=PACK, j=PACK)
+        def dealt(flat):
+            return flat.rearrange("p (t m j) -> p m t j", t=PACK, j=PACK)
 
         def by_column(raw):
             return raw[:].rearrange("p j (m t) -> p m t j", t=PACK)
@@ -65,130 +69,160 @@ def tile_picked_wpna_none_lo_kernel(
         w1_b = sb.tile([P, PACK * T], BF16, align_bytes=64)
         w1_codes = sb.tile([P, T], U32, align_bytes=64)
         w1_plane = sb.tile([P, T], U8, align_bytes=64)
-        for a in range(2):
-            nc.vector.tensor_copy(out=dealt(w1_b)[:, a * 64 : (a + 1) * 64], in_=by_column(w1_raw[a]))
-        h = []
+        nc.vector.tensor_copy(out=dealt(w1_b[:])[:, 0:64], in_=by_column(w1_raw[0]))
+        nc.vector.tensor_copy(out=dealt(w1_b[:])[:, 64 : 64 + VECTOR_M], in_=by_column(w1_raw[1])[:, 0:VECTOR_M])
+        nc.scalar.copy(out=dealt(w1_b[:])[:, 64 + VECTOR_M : P], in_=by_column(w1_raw[1])[:, VECTOR_M:64])
         for t in range(PACK):
             cols = slice(t * P, (t + 1) * P)
             nc.vector.quantize_mx(out=w1_codes[:, cols].bitcast(FP8X4), scales=w1_plane[:, cols], in_=w1_b[:, t * T : (t + 1) * T])
-            acc = bank(t, [P, T], f"h_acc{t}")
-            nc.tensor.matmul_mx(out=acc[:], lhsT=w1_codes[:, cols].bitcast(FP8X4), lhsT_scale=w1_plane[:, cols],
-                                rhs=x_codes[:].bitcast(FP8X4), rhs_scale=x_plane[:], start=True, stop=True)
-            h_t = sb.tile([P, T], F32, name=f"h{t}")
-            nc.scalar.copy(out=h_t[:], in_=acc[:])
-            h.append(h_t)
+        for t in range(PACK):
+            cols = slice(t * P, (t + 1) * P)
+            pieces = [(0, 0, HALF), (4, HALF, T)] if t == 0 else [(t, 0, T)]
+            for b, n0, n1 in pieces:
+                acc = bank(b, [P, n1 - n0], f"h_acc{t}{b}")
+                nc.tensor.matmul_mx(out=acc[:], lhsT=w1_codes[:, cols].bitcast(FP8X4), lhsT_scale=w1_plane[:, cols],
+                                    rhs=x_codes[:, n0:n1].bitcast(FP8X4), rhs_scale=x_plane[:, n0:n1], start=True, stop=True)
+                if n0 == 0:
+                    nc.scalar.copy(out=h[t][:, n0:n1], in_=acc[:])
+                else:
+                    nc.vector.tensor_copy(out=h[t][:, n0:n1], in_=acc[:])
 
-        g = {}
+        g = [sb.tile([P, PACK, T], F32, name=f"g{d}") for d in range(D - 1)]
+        g_last = [sb.tile([P, PACK, HALF], F32, name=f"g_last{c}") for c in range(2)]
+        for d in range(D - 1):
+            for t in range(PACK):
+                nc.vector.tensor_copy(g[d][:, t, :], h[t][:].indirect(lists[d][:]))
         for c in range(2):
-            for d in range(D):
-                g[c, d] = sb.tile([P, PACK, CHUNK], F32, name=f"g{c}{d}")
-                for t in range(PACK):
-                    nc.vector.tensor_copy(g[c, d][:, t, :], h[t][:].indirect(lists[d][:, c * 16 : (c + 1) * 16]))
+            for t in range(PACK):
+                nc.vector.tensor_copy(g_last[c][:, t, :], h[t][:].indirect(lists[D - 1][:, c * 16 : (c + 1) * 16]))
 
-        w_b = [sb.tile([P, PACK * T], BF16, name=f"w_b{k}", align_bytes=64) for k in range(3)]
-        w_codes = [sb.tile([P, T], U32, name=f"w_codes{k}", align_bytes=64) for k in range(3)]
-        w_plane = [sb.tile([P, T], U8, name=f"w_plane{k}", align_bytes=64) for k in range(3)]
-        g_b = [sb.tile([P, D, CHUNK * PACK], BF16, name=f"g_b{c}", align_bytes=64) for c in range(2)]
-        z_b = [[sb.tile([P, CHUNK * PACK], BF16, name=f"z_b{c}{k}", align_bytes=64) for k in range(3)] for c in range(2)]
-        z_codes = [sb.tile([P, T], U32, name=f"z_codes{k}", align_bytes=64) for k in range(3)]
-        z_plane = [sb.tile([P, T], U8, name=f"z_plane{k}", align_bytes=64) for k in range(3)]
+        w_b = sb.tile([P, 3 * PACK * T], BF16, align_bytes=64)
+        w_codes = sb.tile([P, 3 * T], U32, align_bytes=64)
+        w_plane = sb.tile([P, 3 * T], U8, align_bytes=64)
+        g_b = sb.tile([P, D, T * PACK], BF16, align_bytes=64)
+        parts = [(0, HALF), (HALF, BLOCK), (HALF + BLOCK, BLOCK)]
+        mean_b = [sb.tile([P, HALF * PACK], BF16, name=f"mean_b{c}", align_bytes=64) for c in range(2)]
+        ext_b = [sb.tile([P, 2, n * PACK], BF16, name=f"ext_b{i}", align_bytes=64) for i, (v0, n) in enumerate(parts)]
+        z_codes = [sb.tile([P, 3 * n], U32, name=f"z_codes{i}", align_bytes=64) for i, (v0, n) in enumerate(parts)]
+        z_plane = [sb.tile([P, 3 * n], U8, name=f"z_plane{i}", align_bytes=64) for i, (v0, n) in enumerate(parts)]
 
-        def round_weight(k):
-            nc.scalar.copy(out=dealt(w_b[k]), in_=by_column(w_raw[k]))
+        def round_gathered(dst, src):
+            nc.scalar.copy(out=dst.rearrange("p (n i t) -> p n t i", t=PACK, i=4), in_=src.rearrange("p t (n i) -> p n t i", i=4))
 
-        def round_gathered(c, d):
-            nc.scalar.copy(out=g_b[c][:, d, :].rearrange("p (n i t) -> p n t i", t=PACK, i=4),
-                           in_=g[c, d][:].rearrange("p t (n i) -> p n t i", i=4))
+        sums = [bank(4 + j, [P, PACK, P], f"sum{j}") for j in range(4)]
 
-        def sum_turned(c):
-            sums = [bank(4 + 2 * c + b, [P, PACK, P], f"sum{c}{b}") for b in range(2)]
-            for d in range(D):
-                for t in range(PACK):
-                    for b in range(2):
-                        nc.tensor.matmul(sums[b][:, t, :], g[c, d][:, t, b * BLOCK : (b + 1) * BLOCK], ident[:], is_transpose=True,
-                                         start=(d == 0 and t == 0), stop=(d == D - 1 and t == PACK - 1))
-            return sums
+        def add_turned(src, j, t, first, last):
+            nc.tensor.matmul(sums[j][:, t, :], src, ident[:], is_transpose=True, start=first, stop=last)
 
-        def mean_back(c, sums):
+        for d in range(D - 1):
+            for t in range(PACK):
+                for j in range(4):
+                    add_turned(g[d][:, t, j * BLOCK : (j + 1) * BLOCK], j, t, d == 0 and t == 0, False)
+        for c in range(2):
+            for t in range(PACK):
+                for b in range(2):
+                    add_turned(g_last[c][:, t, b * BLOCK : (b + 1) * BLOCK], 2 * c + b, t, False, t == PACK - 1)
+
+        def mean_back(c):
             back = bank(c, [P, 2, 2, BLOCK], f"back{c}")
             for b in range(2):
                 mean_t = sb.tile([P, 2 * P * 2], BF16, name=f"mean_t{c}{b}")
                 nc.scalar.activation(mean_t[:].rearrange("v (u p e) -> v u p e", u=2, e=2),
-                                     sums[b][:].rearrange("v (u e) p -> v u p e", e=2), COPY, scale=0.25)
+                                     sums[2 * c + b][:].rearrange("v (u e) p -> v u p e", e=2), COPY, scale=0.25)
                 words = mean_t[:].bitcast(F32)
                 for u in range(2):
                     nc.tensor.transpose(back[:, b, u, :], words[:, u * P : (u + 1) * P], ident[:])
-            nc.scalar.copy(out=z_b[c][0][:].bitcast(F32).rearrange("p (b v u) -> p b v u", b=2, u=2),
+            nc.scalar.copy(out=mean_b[c][:].bitcast(F32).rearrange("p (b v u) -> p b v u", b=2, u=2),
                            in_=back[:].rearrange("p b u v -> p b v u"))
 
-        sums0 = sum_turned(0)
-        sums1 = sum_turned(1)
-        round_weight(0)
-        round_gathered(0, 0)
-        round_gathered(0, 1)
-        round_weight(1)
-        round_gathered(0, 2)
-        round_gathered(0, 3)
-        mean_back(0, sums0)
-        round_weight(2)
-        for d in range(D):
-            round_gathered(1, d)
-        mean_back(1, sums1)
+        for k in range(3):
+            nc.scalar.copy(out=dealt(w_b[:, k * PACK * T : (k + 1) * PACK * T]), in_=by_column(w_raw[k]))
+        for d in range(D - 1):
+            round_gathered(g_b[:, d, :], g[d][:])
+        for c in range(2):
+            round_gathered(g_b[:, D - 1, c * HALF * PACK : (c + 1) * HALF * PACK], g_last[c][:])
+            mean_back(c)
+
+        def quantize(codes, plane, c0, c1, src):
+            nc.vector.quantize_mx(out=codes[:, c0:c1].bitcast(FP8X4), scales=plane[:, c0:c1], in_=src)
 
         def first_level(c):
+            span = slice(c * HALF * PACK, (c + 1) * HALF * PACK)
             pair = []
             for op, name in ((MAX, "hi"), (MIN, "lo")):
-                two = sb.tile([P, 2, CHUNK * PACK], BF16, name=f"{name}{c}", align_bytes=64)
-                nc.vector.tensor_tensor(two[:], g_b[c][:, 0:2, :], g_b[c][:, 2:4, :], op)
+                two = sb.tile([P, 2, HALF * PACK], BF16, name=f"{name}{c}", align_bytes=64)
+                nc.vector.tensor_tensor(two[:], g_b[:, 0:2, span], g_b[:, 2:4, span], op)
                 pair.append(two)
             return pair
 
-        def statistics(c, pair, v0, n):
-            span = slice((v0 - c * CHUNK) * PACK, (v0 - c * CHUNK + n) * PACK)
-            for k, op in ((1, MAX), (2, MIN)):
-                nc.vector.tensor_tensor(z_b[c][k][:, span], pair[k - 1][:, 0, span], pair[k - 1][:, 1, span], op)
-            for k in range(3):
-                nc.vector.quantize_mx(out=z_codes[k][:, v0 : v0 + n].bitcast(FP8X4), scales=z_plane[k][:, v0 : v0 + n], in_=z_b[c][k][:, span])
+        def statistics(i, pair):
+            v0, n = parts[i]
+            c = v0 // HALF
+            span = slice((v0 - c * HALF) * PACK, (v0 - c * HALF + n) * PACK)
+            for e, op in enumerate((MAX, MIN)):
+                nc.vector.tensor_tensor(ext_b[i][:, e, :], pair[e][:, 0, span], pair[e][:, 1, span], op)
+            quantize(z_codes[i], z_plane[i], 0, n, mean_b[c][:, span])
+            if i < 2:
+                quantize(z_codes[i], z_plane[i], n, 3 * n, ext_b[i][:].rearrange("p e n -> p (e n)"))
+            else:
+                for e in range(2):
+                    quantize(z_codes[i], z_plane[i], (1 + e) * n, (2 + e) * n, ext_b[i][:, e, :])
 
-        y = sb.tile([P, PACK, T], F32)
+        y = [sb.tile([P, PACK, n], F32, name=f"y{i}") for i, (v0, n) in enumerate(parts)]
         y_b = sb.tile([P, T * PACK], BF16, align_bytes=64)
         y_codes = sb.tile([P, T], U32, align_bytes=64)
         y_plane = sb.tile([P, T], U8, align_bytes=64)
         out_rows = out_0.rearrange("(p t) v -> p t v", t=PACK)
         out_words = out_1[0].rearrange("p n t -> p (n t)").bitcast(I32)
 
-        def product(j):
-            cols = slice(j * BLOCK, (j + 1) * BLOCK)
-            acc = bank((2, 3, 4, 5)[j], [P, PACK, BLOCK], f"y_acc{j}")
-            for t in range(PACK):
-                m = slice(t * P, (t + 1) * P)
-                for k in range(3):
-                    nc.tensor.matmul_mx(out=acc[:, t, :], lhsT=w_codes[k][:, m].bitcast(FP8X4), lhsT_scale=w_plane[k][:, m],
-                                        rhs=z_codes[k][:, cols].bitcast(FP8X4), rhs_scale=z_plane[k][:, cols],
-                                        start=(k == 0), stop=(k == 2))
-            nc.scalar.copy(out=y_b[:, j * BLOCK * PACK : (j + 1) * BLOCK * PACK].rearrange("p (v t) -> p v t", t=PACK),
-                           in_=acc[:].rearrange("p t v -> p v t"))
-            nc.scalar.copy(out=y[:, :, cols], in_=acc[:])
+        def one_pass(acc, i, b, t, k, start, stop):
+            n = parts[i][1]
+            m = slice(k * T + t * P, k * T + (t + 1) * P)
+            cols = slice(k * n + b * BLOCK, k * n + (b + 1) * BLOCK)
+            nc.tensor.matmul_mx(out=acc, lhsT=w_codes[:, m].bitcast(FP8X4), lhsT_scale=w_plane[:, m],
+                                rhs=z_codes[i][:, cols].bitcast(FP8X4), rhs_scale=z_plane[i][:, cols], start=start, stop=stop)
 
-        def hand_out(v0, n):
+        def product(i, b, at):
+            v0 = parts[i][0] + b * BLOCK
+            acc = bank(at, [P, PACK, BLOCK], f"y_acc{i}{b}")
+            for t in range(PACK):
+                for k in range(3):
+                    one_pass(acc[:, t, :], i, b, t, k, k == 0, k == 2)
+            nc.scalar.copy(out=y_b[:, v0 * PACK : (v0 + BLOCK) * PACK].rearrange("p (v t) -> p v t", t=PACK),
+                           in_=acc[:].rearrange("p t v -> p v t"))
+            nc.scalar.copy(out=y[i][:, :, b * BLOCK : (b + 1) * BLOCK], in_=acc[:])
+
+        def last_product(i):
+            v0 = parts[i][0]
+            acc = [bank(5 + u, [P, 2, BLOCK], f"y_last{u}") for u in range(2)]
+            for k in range(3):
+                for t in range(PACK):
+                    one_pass(acc[t // 2][:, t % 2, :], i, 0, t, k, k == 0 and t % 2 == 0, k == 2 and t % 2 == 1)
+            nc.scalar.copy(out=y[i][:, 0:2, :], in_=acc[0][:])
+            nc.vector.tensor_copy(out=y[i][:, 2:4, :], in_=acc[1][:])
+            nc.vector.tensor_copy(out=y_b[:, v0 * PACK : (v0 + BLOCK) * PACK].rearrange("p (n j t) -> p n t j", t=PACK, j=4),
+                                  in_=y[i][:].rearrange("p t (n j) -> p n t j", j=4))
+
+        def hand_out(i):
+            v0, n = parts[i]
             cols = slice(v0, v0 + n)
-            nc.sync.dma_start(out=out_rows[:, :, cols], in_=y[:, :, cols])
-            nc.vector.quantize_mx(out=y_codes[:, cols].bitcast(FP8X4), scales=y_plane[:, cols], in_=y_b[:, v0 * PACK : (v0 + n) * PACK])
+            nc.sync.dma_start(out=out_rows[:, :, cols], in_=y[i][:])
+            quantize(y_codes, y_plane, v0, v0 + n, y_b[:, v0 * PACK : (v0 + n) * PACK])
             nc.sync.dma_start(out=out_words[:, cols], in_=y_codes[:, cols].bitcast(I32))
 
-        pair0 = first_level(0)
-        for k in range(3):
-            nc.vector.quantize_mx(out=w_codes[k][:].bitcast(FP8X4), scales=w_plane[k][:], in_=w_b[k][:])
-        statistics(0, pair0, 0, CHUNK)
-        product(0)
-        product(1)
-        pair1 = first_level(1)
-        statistics(1, pair1, 256, BLOCK)
-        product(2)
-        hand_out(0, CHUNK)
-        statistics(1, pair1, 384, BLOCK)
-        product(3)
-        hand_out(256, BLOCK)
-        hand_out(384, BLOCK)
+        quantize(w_codes, w_plane, 0, 2 * T, w_b[:, 0 : 2 * PACK * T])
+        quantize(w_codes, w_plane, 2 * T, 3 * T, w_b[:, 2 * PACK * T :])
+        statistics(0, first_level(0))
+        product(0, 0, 2)
+        product(0, 1, 3)
+        pair = first_level(1)
+        statistics(1, pair)
+        product(1, 0, 4)
+        hand_out(0)
+        statistics(2, pair)
+        hand_out(1)
+        last_product(2)
+        hand_out(2)
         for q in range(4):
-            nc.sync.dma_start(out=out_2[0, 4 * q : 4 * q + 4, :].bitcast(I32), in_=y_plane[32 * q : 32 * q + 4, :].bitcast(I32))
+            queue = nc.sync if q < 2 else nc.scalar
+            queue.dma_start(out=out_2[0, 4 * q : 4 * q + 4, :].bitcast(I32), in_=y_plane[32 * q : 32 * q + 4, :].bitcast(I32))

@@ -61,17 +61,17 @@ def tile_picked_wpna_none_lo_kernel(
         make_identity(nc, ident[:])
 
         def dealt(flat):
-            return flat.rearrange("p (t m j) -> p m t j", t=PACK, j=PACK)
+            return flat.rearrange("p (u e m j) -> p u m j e", u=2, e=2, j=PACK)
 
         def by_column(raw):
-            return raw[:].rearrange("p j (m t) -> p m t j", t=PACK)
+            return raw[:].rearrange("p j (m u e) -> p u m j e", u=2, e=2)
 
         w1_b = sb.tile([P, PACK * T], BF16, align_bytes=64)
         w1_codes = sb.tile([P, T], U32, align_bytes=64)
         w1_plane = sb.tile([P, T], U8, align_bytes=64)
-        nc.vector.tensor_copy(out=dealt(w1_b[:])[:, 0:64], in_=by_column(w1_raw[0]))
-        nc.vector.tensor_copy(out=dealt(w1_b[:])[:, 64 : 64 + VECTOR_M], in_=by_column(w1_raw[1])[:, 0:VECTOR_M])
-        nc.scalar.copy(out=dealt(w1_b[:])[:, 64 + VECTOR_M : P], in_=by_column(w1_raw[1])[:, VECTOR_M:64])
+        nc.vector.tensor_copy(out=dealt(w1_b[:])[:, :, 0:64], in_=by_column(w1_raw[0]))
+        nc.vector.tensor_copy(out=dealt(w1_b[:])[:, :, 64 : 64 + VECTOR_M], in_=by_column(w1_raw[1])[:, :, 0:VECTOR_M])
+        nc.scalar.copy(out=dealt(w1_b[:])[:, :, 64 + VECTOR_M : P], in_=by_column(w1_raw[1])[:, :, VECTOR_M:64])
         for t in range(PACK):
             cols = slice(t * P, (t + 1) * P)
             nc.vector.quantize_mx(out=w1_codes[:, cols].bitcast(FP8X4), scales=w1_plane[:, cols], in_=w1_b[:, t * T : (t + 1) * T])
@@ -107,7 +107,7 @@ def tile_picked_wpna_none_lo_kernel(
         z_plane = [sb.tile([P, 3 * n], U8, name=f"z_plane{i}", align_bytes=64) for i, (v0, n) in enumerate(parts)]
 
         def round_gathered(dst, src):
-            nc.scalar.copy(out=dst.rearrange("p (n i t) -> p n t i", t=PACK, i=4), in_=src.rearrange("p t (n i) -> p n t i", i=4))
+            nc.scalar.copy(out=dst.rearrange("p (n i t) -> p n t i", t=PACK, i=2), in_=src.rearrange("p t (n i) -> p n t i", i=2))
 
         sums = [bank(4 + j, [P, PACK, P], f"sum{j}") for j in range(4)]
 
@@ -200,8 +200,8 @@ def tile_picked_wpna_none_lo_kernel(
                     one_pass(acc[t // 2][:, t % 2, :], i, 0, t, k, k == 0 and t % 2 == 0, k == 2 and t % 2 == 1)
             nc.scalar.copy(out=y[i][:, 0:2, :], in_=acc[0][:])
             nc.vector.tensor_copy(out=y[i][:, 2:4, :], in_=acc[1][:])
-            nc.vector.tensor_copy(out=y_b[:, v0 * PACK : (v0 + BLOCK) * PACK].rearrange("p (n j t) -> p n t j", t=PACK, j=4),
-                                  in_=y[i][:].rearrange("p t (n j) -> p n t j", j=4))
+            nc.vector.tensor_copy(out=y_b[:, v0 * PACK : (v0 + BLOCK) * PACK].rearrange("p (n j t) -> p n t j", t=PACK, j=2),
+                                  in_=y[i][:].rearrange("p t (n j) -> p n t j", j=2))
 
         def hand_out(i):
             v0, n = parts[i]

@@ -42,7 +42,7 @@ def tile_picked_wpna_none_lo_kernel(
         x_plane = sb.tile([P, T], U8, align_bytes=64)
         ident = sb.tile([P, P], F32)
         w1_raw = [sb.tile([P, PACK, HALF], F32, name=f"w1_raw{a}") for a in range(2)]
-        w_raw = [sb.tile([P, PACK, T], F32, name=f"w_raw{k}") for k in range(3)]
+        w_raw = [sb.tile([P, PACK, T], F32, name=f"w_raw{k}", tag=f"w_raw{k}", align_bytes=64) for k in range(3)]
         h = [sb.tile([P, WINDOW], F32, name=f"h{t}") for t in range(PACK)]
 
         nc.vector.memset(x_plane[:].bitcast(U32), 0)
@@ -99,7 +99,6 @@ def tile_picked_wpna_none_lo_kernel(
         w_b = sb.tile([P, 3 * PACK * T], BF16, align_bytes=64)
         w_codes = sb.tile([P, 3 * T], U32, align_bytes=64)
         w_plane = sb.tile([P, 3 * T], U8, align_bytes=64)
-        g_b = sb.tile([P, D, T * PACK], BF16, align_bytes=64)
         parts = [(0, HALF), (HALF, BLOCK), (HALF + BLOCK, BLOCK)]
         mean_b = [sb.tile([P, HALF * PACK], BF16, name=f"mean_b{c}", align_bytes=64) for c in range(2)]
         ext_b = [sb.tile([P, 2, n * PACK], BF16, name=f"ext_b{i}", align_bytes=64) for i, (v0, n) in enumerate(parts)]
@@ -137,10 +136,11 @@ def tile_picked_wpna_none_lo_kernel(
 
         for k in range(3):
             nc.scalar.copy(out=dealt(w_b[:, k * PACK * T : (k + 1) * PACK * T]), in_=by_column(w_raw[k]))
+        g_b = [sb.tile([P, 2, T * PACK], BF16, name=f"g_b{e}", tag=f"w_raw{e + 1}", align_bytes=64) for e in range(2)]
         for d in range(D - 1):
-            round_gathered(g_b[:, d, :], g[d][:])
+            round_gathered(g_b[d // 2][:, d % 2, :], g[d][:])
         for c in range(2):
-            round_gathered(g_b[:, D - 1, c * HALF * PACK : (c + 1) * HALF * PACK], g_last[c][:])
+            round_gathered(g_b[1][:, 1, c * HALF * PACK : (c + 1) * HALF * PACK], g_last[c][:])
             mean_back(c)
 
         def quantize(codes, plane, c0, c1, src):
@@ -151,7 +151,7 @@ def tile_picked_wpna_none_lo_kernel(
             pair = []
             for op, name in ((MAX, "hi"), (MIN, "lo")):
                 two = sb.tile([P, 2, HALF * PACK], BF16, name=f"{name}{c}", align_bytes=64)
-                nc.vector.tensor_tensor(two[:], g_b[:, 0:2, span], g_b[:, 2:4, span], op)
+                nc.vector.tensor_tensor(two[:], g_b[0][:, :, span], g_b[1][:, :, span], op)
                 pair.append(two)
             return pair
 
@@ -203,26 +203,35 @@ def tile_picked_wpna_none_lo_kernel(
             nc.vector.tensor_copy(out=y_b[:, v0 * PACK : (v0 + BLOCK) * PACK].rearrange("p (n j t) -> p n t j", t=PACK, j=2),
                                   in_=y[i][:].rearrange("p t (n j) -> p n t j", j=2))
 
-        def hand_out(i):
+        def store_result(i):
             v0, n = parts[i]
-            cols = slice(v0, v0 + n)
-            nc.sync.dma_start(out=out_rows[:, :, cols], in_=y[i][:])
+            nc.sync.dma_start(out=out_rows[:, :, v0 : v0 + n], in_=y[i][:])
+
+        def quantize_result(i):
+            v0, n = parts[i]
             quantize(y_codes, y_plane, v0, v0 + n, y_b[:, v0 * PACK : (v0 + n) * PACK])
-            nc.sync.dma_start(out=out_words[:, cols], in_=y_codes[:, cols].bitcast(I32))
+
+        def store_words(v0, v1):
+            nc.sync.dma_start(out=out_words[:, v0:v1], in_=y_codes[:, v0:v1].bitcast(I32))
 
         quantize(w_codes, w_plane, 0, 2 * T, w_b[:, 0 : 2 * PACK * T])
         quantize(w_codes, w_plane, 2 * T, 3 * T, w_b[:, 2 * PACK * T :])
         statistics(0, first_level(0))
         product(0, 0, 2)
         product(0, 1, 3)
+        store_result(0)
         pair = first_level(1)
         statistics(1, pair)
         product(1, 0, 4)
-        hand_out(0)
+        store_result(1)
         statistics(2, pair)
-        hand_out(1)
+        quantize_result(0)
+        quantize_result(1)
+        store_words(0, T - BLOCK)
         last_product(2)
-        hand_out(2)
+        store_result(2)
+        quantize_result(2)
+        store_words(T - BLOCK, T)
         for q in range(4):
             queue = nc.sync if q < 2 else nc.scalar
             queue.dma_start(out=out_2[0, 4 * q : 4 * q + 4, :].bitcast(I32), in_=y_plane[32 * q : 32 * q + 4, :].bitcast(I32))

@@ -20,10 +20,12 @@ P = 128
 PACK = 4
 T = 512
 D = 4
-HALF = 256
+STATS = 3
+QUADRANTS = 4
+HALF = T // 2
 BLOCK = 128
+LIST_ROWS = 16
 WINDOW = 704
-VECTOR_M = 40
 
 
 def tile_picked_wpna_none_lo_kernel(
@@ -34,20 +36,25 @@ def tile_picked_wpna_none_lo_kernel(
         sb = ctx.enter_context(tc.tile_pool(name="sb", bufs=1))
         ps = ctx.enter_context(tc.psum_pool(name="ps", bufs=1))
 
-        def bank(b, shape, name):
-            return ps.tile(shape, F32, name=name, tag=f"bank{b}")
+        def bank(number, shape, name):
+            return ps.tile(shape, F32, name=name, tag=f"bank{number}")
 
-        lists = [sb.tile([P, T // 16], U16, name=f"list{d}") for d in range(D)]
+        def quantize(codes, plane, c0, c1, src):
+            nc.vector.quantize_mx(out=codes[:, c0:c1].bitcast(FP8X4), scales=plane[:, c0:c1], in_=src)
+
+        lists = [sb.tile([P, T // LIST_ROWS], U16, name=f"list{d}") for d in range(D)]
         x_codes = sb.tile([P, T], U32, align_bytes=64)
         x_plane = sb.tile([P, T], U8, align_bytes=64)
         ident = sb.tile([P, P], F32)
         w1_raw = [sb.tile([P, PACK, HALF], F32, name=f"w1_raw{a}") for a in range(2)]
-        w_raw = [sb.tile([P, PACK, T], F32, name=f"w_raw{k}", tag=f"w_raw{k}", align_bytes=64) for k in range(3)]
+        w_raw = [sb.tile([P, PACK, T], F32, name=f"w_raw{k}", tag=f"w_raw{k}", align_bytes=64) for k in range(STATS)]
         h = [sb.tile([P, WINDOW], F32, name=f"h{t}") for t in range(PACK)]
 
         nc.vector.memset(x_plane[:].bitcast(U32), 0)
-        for q in range(4):
-            nc.scalar.dma_start(out=x_plane[32 * q : 32 * q + 4, :].bitcast(I32), in_=x_scales[0, 4 * q : 4 * q + 4, :].bitcast(I32))
+        for q in range(QUADRANTS):
+            nc.scalar.dma_start(
+                out=x_plane[32 * q : 32 * q + 4, :].bitcast(I32), in_=x_scales[0, 4 * q : 4 * q + 4, :].bitcast(I32)
+            )
         w1_rows = w1.rearrange("(p j) c -> p j c", j=PACK)
         for a in range(2):
             nc.sync.dma_start(out=w1_raw[a][:], in_=w1_rows[:, :, a * HALF : (a + 1) * HALF])
@@ -69,53 +76,55 @@ def tile_picked_wpna_none_lo_kernel(
         w1_b = sb.tile([P, PACK * T], BF16, align_bytes=64)
         w1_codes = sb.tile([P, T], U32, align_bytes=64)
         w1_plane = sb.tile([P, T], U8, align_bytes=64)
-        nc.vector.tensor_copy(out=dealt(w1_b[:])[:, :, 0:64], in_=by_column(w1_raw[0]))
-        nc.vector.tensor_copy(out=dealt(w1_b[:])[:, :, 64 : 64 + VECTOR_M], in_=by_column(w1_raw[1])[:, :, 0:VECTOR_M])
-        nc.scalar.copy(out=dealt(w1_b[:])[:, :, 64 + VECTOR_M : P], in_=by_column(w1_raw[1])[:, :, VECTOR_M:64])
+        nc.vector.tensor_copy(out=dealt(w1_b[:])[:, :, 0 : P // 2], in_=by_column(w1_raw[0]))
+        nc.vector.tensor_copy(out=dealt(w1_b[:])[:, 0, P // 2 : P], in_=by_column(w1_raw[1])[:, 0])
+        nc.scalar.copy(out=dealt(w1_b[:])[:, 1, P // 2 : P], in_=by_column(w1_raw[1])[:, 1])
         for t in range(PACK):
+            quantize(w1_codes, w1_plane, t * P, (t + 1) * P, w1_b[:, t * T : (t + 1) * T])
+
+        def project(t, number, n0, n1, copy_out):
             cols = slice(t * P, (t + 1) * P)
-            nc.vector.quantize_mx(out=w1_codes[:, cols].bitcast(FP8X4), scales=w1_plane[:, cols], in_=w1_b[:, t * T : (t + 1) * T])
-        for t in range(PACK):
-            cols = slice(t * P, (t + 1) * P)
-            pieces = [(0, 0, HALF), (4, HALF, T)] if t == 0 else [(t, 0, T)]
-            for b, n0, n1 in pieces:
-                acc = bank(b, [P, n1 - n0], f"h_acc{t}{b}")
-                nc.tensor.matmul_mx(out=acc[:], lhsT=w1_codes[:, cols].bitcast(FP8X4), lhsT_scale=w1_plane[:, cols],
-                                    rhs=x_codes[:, n0:n1].bitcast(FP8X4), rhs_scale=x_plane[:, n0:n1], start=True, stop=True)
-                if n0 == 0:
-                    nc.scalar.copy(out=h[t][:, n0:n1], in_=acc[:])
-                else:
-                    nc.vector.tensor_copy(out=h[t][:, n0:n1], in_=acc[:])
+            acc = bank(number, [P, n1 - n0], f"h_acc{t}{number}")
+            nc.tensor.matmul_mx(
+                out=acc[:], lhsT=w1_codes[:, cols].bitcast(FP8X4), lhsT_scale=w1_plane[:, cols],
+                rhs=x_codes[:, n0:n1].bitcast(FP8X4), rhs_scale=x_plane[:, n0:n1], start=True, stop=True,
+            )
+            copy_out(out=h[t][:, n0:n1], in_=acc[:])
+
+        project(0, 0, 0, HALF, nc.scalar.copy)
+        project(0, PACK, HALF, T, nc.vector.tensor_copy)
+        for t in range(1, PACK):
+            project(t, t, 0, T, nc.scalar.copy)
 
         g = [sb.tile([P, PACK, T], F32, name=f"g{d}") for d in range(D - 1)]
         g_last = [sb.tile([P, PACK, HALF], F32, name=f"g_last{c}") for c in range(2)]
         for d in range(D - 1):
             for t in range(PACK):
                 nc.vector.tensor_copy(g[d][:, t, :], h[t][:].indirect(lists[d][:]))
+        half_columns = HALF // LIST_ROWS
         for c in range(2):
             for t in range(PACK):
-                nc.vector.tensor_copy(g_last[c][:, t, :], h[t][:].indirect(lists[D - 1][:, c * 16 : (c + 1) * 16]))
+                offsets = lists[D - 1][:, c * half_columns : (c + 1) * half_columns]
+                nc.vector.tensor_copy(g_last[c][:, t, :], h[t][:].indirect(offsets))
 
-        w_b = sb.tile([P, 3 * PACK * T], BF16, align_bytes=64)
-        w_codes = sb.tile([P, 3 * T], U32, align_bytes=64)
-        w_plane = sb.tile([P, 3 * T], U8, align_bytes=64)
         parts = [(0, HALF), (HALF, BLOCK), (HALF + BLOCK, BLOCK)]
+        last_part = len(parts) - 1
+        w_b = sb.tile([P, STATS * PACK * T], BF16, align_bytes=64)
+        w_codes = sb.tile([P, STATS * T], U32, align_bytes=64)
+        w_plane = sb.tile([P, STATS * T], U8, align_bytes=64)
         mean_b = [sb.tile([P, HALF * PACK], BF16, name=f"mean_b{c}", align_bytes=64) for c in range(2)]
         ext_b = [sb.tile([P, 2, n * PACK], BF16, name=f"ext_b{i}", align_bytes=64) for i, (v0, n) in enumerate(parts)]
-        z_codes = [sb.tile([P, 3 * n], U32, name=f"z_codes{i}", align_bytes=64) for i, (v0, n) in enumerate(parts)]
-        z_plane = [sb.tile([P, 3 * n], U8, name=f"z_plane{i}", align_bytes=64) for i, (v0, n) in enumerate(parts)]
+        z_codes = [sb.tile([P, STATS * n], U32, name=f"z_codes{i}", align_bytes=64) for i, (v0, n) in enumerate(parts)]
+        z_plane = [sb.tile([P, STATS * n], U8, name=f"z_plane{i}", align_bytes=64) for i, (v0, n) in enumerate(parts)]
 
-        def round_gathered(dst, src):
-            nc.scalar.copy(out=dst.rearrange("p (n i t) -> p n t i", t=PACK, i=2), in_=src.rearrange("p t (n i) -> p n t i", i=2))
-
-        sums = [bank(4 + j, [P, PACK, P], f"sum{j}") for j in range(4)]
+        sums = [bank(PACK + j, [P, PACK, P], f"sum{j}") for j in range(T // BLOCK)]
 
         def add_turned(src, j, t, first, last):
             nc.tensor.matmul(sums[j][:, t, :], src, ident[:], is_transpose=True, start=first, stop=last)
 
         for d in range(D - 1):
             for t in range(PACK):
-                for j in range(4):
+                for j in range(T // BLOCK):
                     add_turned(g[d][:, t, j * BLOCK : (j + 1) * BLOCK], j, t, d == 0 and t == 0, False)
         for c in range(2):
             for t in range(PACK):
@@ -125,45 +134,54 @@ def tile_picked_wpna_none_lo_kernel(
         def mean_back(c):
             back = bank(c, [P, 2, 2, BLOCK], f"back{c}")
             for b in range(2):
-                mean_t = sb.tile([P, 2 * P * 2], BF16, name=f"mean_t{c}{b}")
-                nc.scalar.activation(mean_t[:].rearrange("v (u p e) -> v u p e", u=2, e=2),
-                                     sums[2 * c + b][:].rearrange("v (u e) p -> v u p e", e=2), COPY, scale=0.25)
-                words = mean_t[:].bitcast(F32)
+                mean_t = sb.tile([P, PACK * P], BF16, name=f"mean_t{c}{b}")
+                nc.scalar.activation(
+                    mean_t[:].rearrange("v (u p e) -> v u p e", u=2, e=2),
+                    sums[2 * c + b][:].rearrange("v (u e) p -> v u p e", e=2), COPY, scale=1.0 / D,
+                )
+                pairs = mean_t[:].bitcast(F32)
                 for u in range(2):
-                    nc.tensor.transpose(back[:, b, u, :], words[:, u * P : (u + 1) * P], ident[:])
-            nc.scalar.copy(out=mean_b[c][:].bitcast(F32).rearrange("p (b v u) -> p b v u", b=2, u=2),
-                           in_=back[:].rearrange("p b u v -> p b v u"))
+                    nc.tensor.transpose(back[:, b, u, :], pairs[:, u * P : (u + 1) * P], ident[:])
+            nc.scalar.copy(
+                out=mean_b[c][:].bitcast(F32).rearrange("p (b v u) -> p b v u", b=2, u=2),
+                in_=back[:].rearrange("p b u v -> p b v u"),
+            )
 
-        for k in range(3):
+        for k in range(STATS):
             nc.scalar.copy(out=dealt(w_b[:, k * PACK * T : (k + 1) * PACK * T]), in_=by_column(w_raw[k]))
-        g_b = [sb.tile([P, 2, T * PACK], BF16, name=f"g_b{e}", tag=f"w_raw{e + 1}", align_bytes=64) for e in range(2)]
+        g_b = [sb.tile([P, 2 * T * PACK], BF16, name=f"g_b{e}", tag=f"w_raw{e + 1}", align_bytes=64) for e in range(2)]
         for d in range(D - 1):
-            round_gathered(g_b[d // 2][:, d % 2, :], g[d][:])
+            nc.scalar.copy(
+                out=g_b[d // 2][:].rearrange("p (c s n i t) -> p s c n t i", c=2, s=2, t=PACK, i=2)[:, d % 2],
+                in_=g[d][:].rearrange("p t (c n i) -> p c n t i", c=2, i=2),
+            )
         for c in range(2):
-            round_gathered(g_b[1][:, 1, c * HALF * PACK : (c + 1) * HALF * PACK], g_last[c][:])
+            nc.scalar.copy(
+                out=g_b[1][:, (2 * c + 1) * HALF * PACK : (2 * c + 2) * HALF * PACK].rearrange(
+                    "p (n i t) -> p n t i", t=PACK, i=2
+                ),
+                in_=g_last[c][:].rearrange("p t (n i) -> p n t i", i=2),
+            )
             mean_back(c)
 
-        def quantize(codes, plane, c0, c1, src):
-            nc.vector.quantize_mx(out=codes[:, c0:c1].bitcast(FP8X4), scales=plane[:, c0:c1], in_=src)
-
         def first_level(c):
-            span = slice(c * HALF * PACK, (c + 1) * HALF * PACK)
-            pair = []
+            span = slice(2 * c * HALF * PACK, (2 * c + 2) * HALF * PACK)
+            halfway = []
             for op, name in ((MAX, "hi"), (MIN, "lo")):
                 two = sb.tile([P, 2, HALF * PACK], BF16, name=f"{name}{c}", align_bytes=64)
-                nc.vector.tensor_tensor(two[:], g_b[0][:, :, span], g_b[1][:, :, span], op)
-                pair.append(two)
-            return pair
+                nc.vector.tensor_tensor(two[:].rearrange("p s n -> p (s n)"), g_b[0][:, span], g_b[1][:, span], op)
+                halfway.append(two)
+            return halfway
 
-        def statistics(i, pair):
+        def statistics(i, halfway):
             v0, n = parts[i]
             c = v0 // HALF
             span = slice((v0 - c * HALF) * PACK, (v0 - c * HALF + n) * PACK)
             for e, op in enumerate((MAX, MIN)):
-                nc.vector.tensor_tensor(ext_b[i][:, e, :], pair[e][:, 0, span], pair[e][:, 1, span], op)
+                nc.vector.tensor_tensor(ext_b[i][:, e, :], halfway[e][:, 0, span], halfway[e][:, 1, span], op)
             quantize(z_codes[i], z_plane[i], 0, n, mean_b[c][:, span])
-            if i < 2:
-                quantize(z_codes[i], z_plane[i], n, 3 * n, ext_b[i][:].rearrange("p e n -> p (e n)"))
+            if i < last_part:
+                quantize(z_codes[i], z_plane[i], n, STATS * n, ext_b[i][:].rearrange("p e n -> p (e n)"))
             else:
                 for e in range(2):
                     quantize(z_codes[i], z_plane[i], (1 + e) * n, (2 + e) * n, ext_b[i][:, e, :])
@@ -177,31 +195,37 @@ def tile_picked_wpna_none_lo_kernel(
 
         def one_pass(acc, i, b, t, k, start, stop):
             n = parts[i][1]
-            m = slice(k * T + t * P, k * T + (t + 1) * P)
+            rows = slice(k * T + t * P, k * T + (t + 1) * P)
             cols = slice(k * n + b * BLOCK, k * n + (b + 1) * BLOCK)
-            nc.tensor.matmul_mx(out=acc, lhsT=w_codes[:, m].bitcast(FP8X4), lhsT_scale=w_plane[:, m],
-                                rhs=z_codes[i][:, cols].bitcast(FP8X4), rhs_scale=z_plane[i][:, cols], start=start, stop=stop)
+            nc.tensor.matmul_mx(
+                out=acc, lhsT=w_codes[:, rows].bitcast(FP8X4), lhsT_scale=w_plane[:, rows],
+                rhs=z_codes[i][:, cols].bitcast(FP8X4), rhs_scale=z_plane[i][:, cols], start=start, stop=stop,
+            )
 
-        def product(i, b, at):
+        def product(i, b, number):
             v0 = parts[i][0] + b * BLOCK
-            acc = bank(at, [P, PACK, BLOCK], f"y_acc{i}{b}")
+            acc = bank(number, [P, PACK, BLOCK], f"y_acc{i}{b}")
             for t in range(PACK):
-                for k in range(3):
-                    one_pass(acc[:, t, :], i, b, t, k, k == 0, k == 2)
-            nc.scalar.copy(out=y_b[:, v0 * PACK : (v0 + BLOCK) * PACK].rearrange("p (v t) -> p v t", t=PACK),
-                           in_=acc[:].rearrange("p t v -> p v t"))
+                for k in range(STATS):
+                    one_pass(acc[:, t, :], i, b, t, k, k == 0, k == STATS - 1)
+            nc.scalar.copy(
+                out=y_b[:, v0 * PACK : (v0 + BLOCK) * PACK].rearrange("p (v t) -> p v t", t=PACK),
+                in_=acc[:].rearrange("p t v -> p v t"),
+            )
             nc.scalar.copy(out=y[i][:, :, b * BLOCK : (b + 1) * BLOCK], in_=acc[:])
 
-        def last_product(i):
+        def last_product(i, numbers):
             v0 = parts[i][0]
-            acc = [bank(5 + u, [P, 2, BLOCK], f"y_last{u}") for u in range(2)]
-            for k in range(3):
+            acc = [bank(number, [P, 2, BLOCK], f"y_last{u}") for u, number in enumerate(numbers)]
+            for k in range(STATS):
                 for t in range(PACK):
-                    one_pass(acc[t // 2][:, t % 2, :], i, 0, t, k, k == 0 and t % 2 == 0, k == 2 and t % 2 == 1)
+                    one_pass(acc[t // 2][:, t % 2, :], i, 0, t, k, k == 0 and t % 2 == 0, k == STATS - 1 and t % 2 == 1)
             nc.scalar.copy(out=y[i][:, 0:2, :], in_=acc[0][:])
             nc.vector.tensor_copy(out=y[i][:, 2:4, :], in_=acc[1][:])
-            nc.vector.tensor_copy(out=y_b[:, v0 * PACK : (v0 + BLOCK) * PACK].rearrange("p (n j t) -> p n t j", t=PACK, j=2),
-                                  in_=y[i][:].rearrange("p t (n j) -> p n t j", j=2))
+            nc.vector.tensor_copy(
+                out=y_b[:, v0 * PACK : (v0 + BLOCK) * PACK].rearrange("p (n i t) -> p n t i", t=PACK, i=2),
+                in_=y[i][:].rearrange("p t (n i) -> p n t i", i=2),
+            )
 
         def store_result(i):
             v0, n = parts[i]
@@ -215,23 +239,25 @@ def tile_picked_wpna_none_lo_kernel(
             nc.sync.dma_start(out=out_words[:, v0:v1], in_=y_codes[:, v0:v1].bitcast(I32))
 
         quantize(w_codes, w_plane, 0, 2 * T, w_b[:, 0 : 2 * PACK * T])
-        quantize(w_codes, w_plane, 2 * T, 3 * T, w_b[:, 2 * PACK * T :])
+        quantize(w_codes, w_plane, 2 * T, STATS * T, w_b[:, 2 * PACK * T :])
         statistics(0, first_level(0))
         product(0, 0, 2)
         product(0, 1, 3)
         store_result(0)
-        pair = first_level(1)
-        statistics(1, pair)
+        second_half = first_level(1)
+        statistics(1, second_half)
         product(1, 0, 4)
         store_result(1)
-        statistics(2, pair)
+        statistics(last_part, second_half)
         quantize_result(0)
         quantize_result(1)
         store_words(0, T - BLOCK)
-        last_product(2)
-        store_result(2)
-        quantize_result(2)
+        last_product(last_part, (5, 6))
+        store_result(last_part)
+        quantize_result(last_part)
         store_words(T - BLOCK, T)
-        for q in range(4):
-            queue = nc.sync if q < 2 else nc.scalar
-            queue.dma_start(out=out_2[0, 4 * q : 4 * q + 4, :].bitcast(I32), in_=y_plane[32 * q : 32 * q + 4, :].bitcast(I32))
+        for q in range(QUADRANTS):
+            queue = nc.sync if q < QUADRANTS // 2 else nc.scalar
+            queue.dma_start(
+                out=out_2[0, 4 * q : 4 * q + 4, :].bitcast(I32), in_=y_plane[32 * q : 32 * q + 4, :].bitcast(I32)
+            )

from contextlib import ExitStack

import concourse.mybir as mybir
from concourse.masks import make_identity

FLOPS = 4 * 2 * 512 * 512 * 512

F32 = mybir.dt.float32
BF16 = mybir.dt.bfloat16
U32 = mybir.dt.uint32
I32 = mybir.dt.int32
U16 = mybir.dt.uint16
U8 = mybir.dt.uint8
FP8X4 = mybir.dt.float8_e4m3fn_x4
MAX = mybir.AluOpType.max
MIN = mybir.AluOpType.min
COPY = mybir.ActivationFunctionType.Copy

P = 128
PACK = 4
T = 512
D = 4
STATS = 3
QUADRANTS = 4
HALF = T // 2
BLOCK = 128
LIST_ROWS = 16
WINDOW = 704


def tile_picked_wpna_none_lo_kernel(
    tc, x_words, x_scales, w1, w2, w3, w4, pos1, pos2, pos3, pos4, out_0, out_1, out_2
):
    nc = tc.nc
    with ExitStack() as ctx:
        sb = ctx.enter_context(tc.tile_pool(name="sb", bufs=1))
        ps = ctx.enter_context(tc.psum_pool(name="ps", bufs=1))

        def bank(number, shape, name):
            return ps.tile(shape, F32, name=name, tag=f"bank{number}")

        def quantize(codes, plane, c0, c1, src):
            nc.vector.quantize_mx(out=codes[:, c0:c1].bitcast(FP8X4), scales=plane[:, c0:c1], in_=src)

        lists = [sb.tile([P, T // LIST_ROWS], U16, name=f"list{d}") for d in range(D)]
        x_codes = sb.tile([P, T], U32, align_bytes=64)
        x_plane = sb.tile([P, T], U8, align_bytes=64)
        ident = sb.tile([P, P], F32)
        w1_raw = [sb.tile([P, PACK, HALF], F32, name=f"w1_raw{a}") for a in range(2)]
        w_raw = [sb.tile([P, PACK, T], F32, name=f"w_raw{k}", tag=f"w_raw{k}", align_bytes=64) for k in range(STATS)]
        h = [sb.tile([P, WINDOW], F32, name=f"h{t}") for t in range(PACK)]

        nc.vector.memset(x_plane[:].bitcast(U32), 0)
        for q in range(QUADRANTS):
            nc.scalar.dma_start(
                out=x_plane[32 * q : 32 * q + 4, :].bitcast(I32), in_=x_scales[0, 4 * q : 4 * q + 4, :].bitcast(I32)
            )
        w1_rows = w1.rearrange("(p j) c -> p j c", j=PACK)
        for a in range(2):
            nc.sync.dma_start(out=w1_raw[a][:], in_=w1_rows[:, :, a * HALF : (a + 1) * HALF])
        nc.sync.dma_start(out=x_codes[:].bitcast(I32), in_=x_words[0].rearrange("p n t -> p (n t)").bitcast(I32))
        for d, pos in enumerate((pos1, pos2, pos3, pos4)):
            nc.sync.dma_start(lists[d][:], pos)
        for k, w in enumerate((w2, w3, w4)):
            nc.sync.dma_start(out=w_raw[k][:], in_=w.rearrange("(p j) c -> p j c", j=PACK))
        for t in range(PACK):
            nc.gpsimd.memset(h[t][:, T:], 0.0)
        make_identity(nc, ident[:])

        def dealt(flat):
            return flat.rearrange("p (u e m j) -> p u m j e", u=2, e=2, j=PACK)

        def by_column(raw):
            return raw[:].rearrange("p j (m u e) -> p u m j e", u=2, e=2)

        w1_b = sb.tile([P, PACK * T], BF16, align_bytes=64)
        w1_codes = sb.tile([P, T], U32, align_bytes=64)
        w1_plane = sb.tile([P, T], U8, align_bytes=64)
        nc.vector.tensor_copy(out=dealt(w1_b[:])[:, :, 0 : P // 2], in_=by_column(w1_raw[0]))
        nc.vector.tensor_copy(out=dealt(w1_b[:])[:, 0, P // 2 : P], in_=by_column(w1_raw[1])[:, 0])
        nc.scalar.copy(out=dealt(w1_b[:])[:, 1, P // 2 : P], in_=by_column(w1_raw[1])[:, 1])
        for t in range(PACK):
            quantize(w1_codes, w1_plane, t * P, (t + 1) * P, w1_b[:, t * T : (t + 1) * T])

        def project(t, number, n0, n1, copy_out):
            cols = slice(t * P, (t + 1) * P)
            acc = bank(number, [P, n1 - n0], f"h_acc{t}{number}")
            nc.tensor.matmul_mx(
                out=acc[:], lhsT=w1_codes[:, cols].bitcast(FP8X4), lhsT_scale=w1_plane[:, cols],
                rhs=x_codes[:, n0:n1].bitcast(FP8X4), rhs_scale=x_plane[:, n0:n1], start=True, stop=True,
            )
            copy_out(out=h[t][:, n0:n1], in_=acc[:])

        project(0, 0, 0, HALF, nc.scalar.copy)
        project(0, PACK, HALF, T, nc.vector.tensor_copy)
        for t in range(1, PACK):
            project(t, t, 0, T, nc.scalar.copy)

        g = [sb.tile([P, PACK, T], F32, name=f"g{d}") for d in range(D - 1)]
        g_last = [sb.tile([P, PACK, HALF], F32, name=f"g_last{c}") for c in range(2)]
        for d in range(D - 1):
            for t in range(PACK):
                nc.vector.tensor_copy(g[d][:, t, :], h[t][:].indirect(lists[d][:]))
        half_columns = HALF // LIST_ROWS
        for c in range(2):
            for t in range(PACK):
                offsets = lists[D - 1][:, c * half_columns : (c + 1) * half_columns]
                nc.vector.tensor_copy(g_last[c][:, t, :], h[t][:].indirect(offsets))

        parts = [(0, HALF), (HALF, BLOCK), (HALF + BLOCK, BLOCK)]
        last_part = len(parts) - 1
        w_b = sb.tile([P, STATS * PACK * T], BF16, align_bytes=64)
        w_codes = sb.tile([P, STATS * T], U32, align_bytes=64)
        w_plane = sb.tile([P, STATS * T], U8, align_bytes=64)
        mean_b = [sb.tile([P, HALF * PACK], BF16, name=f"mean_b{c}", align_bytes=64) for c in range(2)]
        ext_b = [sb.tile([P, 2, n * PACK], BF16, name=f"ext_b{i}", align_bytes=64) for i, (v0, n) in enumerate(parts)]
        z_codes = [sb.tile([P, STATS * n], U32, name=f"z_codes{i}", align_bytes=64) for i, (v0, n) in enumerate(parts)]
        z_plane = [sb.tile([P, STATS * n], U8, name=f"z_plane{i}", align_bytes=64) for i, (v0, n) in enumerate(parts)]

        sums = [bank(PACK + j, [P, PACK, P], f"sum{j}") for j in range(T // BLOCK)]

        def add_turned(src, j, t, first, last):
            nc.tensor.matmul(sums[j][:, t, :], src, ident[:], is_transpose=True, start=first, stop=last)

        for d in range(D - 1):
            for t in range(PACK):
                for j in range(T // BLOCK):
                    add_turned(g[d][:, t, j * BLOCK : (j + 1) * BLOCK], j, t, d == 0 and t == 0, False)
        for c in range(2):
            for t in range(PACK):
                for b in range(2):
                    add_turned(g_last[c][:, t, b * BLOCK : (b + 1) * BLOCK], 2 * c + b, t, False, t == PACK - 1)

        def mean_back(c):
            back = bank(c, [P, 2, 2, BLOCK], f"back{c}")
            for b in range(2):
                mean_t = sb.tile([P, PACK * P], BF16, name=f"mean_t{c}{b}")
                nc.scalar.activation(
                    mean_t[:].rearrange("v (u p e) -> v u p e", u=2, e=2),
                    sums[2 * c + b][:].rearrange("v (u e) p -> v u p e", e=2), COPY, scale=1.0 / D,
                )
                pairs = mean_t[:].bitcast(F32)
                for u in range(2):
                    nc.tensor.transpose(back[:, b, u, :], pairs[:, u * P : (u + 1) * P], ident[:])
            nc.scalar.copy(
                out=mean_b[c][:].bitcast(F32).rearrange("p (b v u) -> p b v u", b=2, u=2),
                in_=back[:].rearrange("p b u v -> p b v u"),
            )

        for k in range(STATS):
            nc.scalar.copy(out=dealt(w_b[:, k * PACK * T : (k + 1) * PACK * T]), in_=by_column(w_raw[k]))
        g_b = [sb.tile([P, 2 * T * PACK], BF16, name=f"g_b{e}", tag=f"w_raw{e + 1}", align_bytes=64) for e in range(2)]
        for d in range(D - 1):
            nc.scalar.copy(
                out=g_b[d // 2][:].rearrange("p (c s n i t) -> p s c n t i", c=2, s=2, t=PACK, i=2)[:, d % 2],
                in_=g[d][:].rearrange("p t (c n i) -> p c n t i", c=2, i=2),
            )
        for c in range(2):
            nc.scalar.copy(
                out=g_b[1][:, (2 * c + 1) * HALF * PACK : (2 * c + 2) * HALF * PACK].rearrange(
                    "p (n i t) -> p n t i", t=PACK, i=2
                ),
                in_=g_last[c][:].rearrange("p t (n i) -> p n t i", i=2),
            )
            mean_back(c)

        def first_level(c):
            span = slice(2 * c * HALF * PACK, (2 * c + 2) * HALF * PACK)
            halfway = []
            for op, name in ((MAX, "hi"), (MIN, "lo")):
                two = sb.tile([P, 2, HALF * PACK], BF16, name=f"{name}{c}", align_bytes=64)
                nc.vector.tensor_tensor(two[:].rearrange("p s n -> p (s n)"), g_b[0][:, span], g_b[1][:, span], op)
                halfway.append(two)
            return halfway

        def statistics(i, halfway):
            v0, n = parts[i]
            c = v0 // HALF
            span = slice((v0 - c * HALF) * PACK, (v0 - c * HALF + n) * PACK)
            for e, op in enumerate((MAX, MIN)):
                nc.vector.tensor_tensor(ext_b[i][:, e, :], halfway[e][:, 0, span], halfway[e][:, 1, span], op)
            quantize(z_codes[i], z_plane[i], 0, n, mean_b[c][:, span])
            if i < last_part:
                quantize(z_codes[i], z_plane[i], n, STATS * n, ext_b[i][:].rearrange("p e n -> p (e n)"))
            else:
                for e in range(2):
                    quantize(z_codes[i], z_plane[i], (1 + e) * n, (2 + e) * n, ext_b[i][:, e, :])

        y = [sb.tile([P, PACK, n], F32, name=f"y{i}") for i, (v0, n) in enumerate(parts)]
        y_b = sb.tile([P, T * PACK], BF16, align_bytes=64)
        y_codes = sb.tile([P, T], U32, align_bytes=64)
        y_plane = sb.tile([P, T], U8, align_bytes=64)
        out_rows = out_0.rearrange("(p t) v -> p t v", t=PACK)
        out_words = out_1[0].rearrange("p n t -> p (n t)").bitcast(I32)

        def one_pass(acc, i, b, t, k, start, stop):
            n = parts[i][1]
            rows = slice(k * T + t * P, k * T + (t + 1) * P)
            cols = slice(k * n + b * BLOCK, k * n + (b + 1) * BLOCK)
            nc.tensor.matmul_mx(
                out=acc, lhsT=w_codes[:, rows].bitcast(FP8X4), lhsT_scale=w_plane[:, rows],
                rhs=z_codes[i][:, cols].bitcast(FP8X4), rhs_scale=z_plane[i][:, cols], start=start, stop=stop,
            )

        def product(i, b, number):
            v0 = parts[i][0] + b * BLOCK
            acc = bank(number, [P, PACK, BLOCK], f"y_acc{i}{b}")
            for t in range(PACK):
                for k in range(STATS):
                    one_pass(acc[:, t, :], i, b, t, k, k == 0, k == STATS - 1)
            nc.scalar.copy(
                out=y_b[:, v0 * PACK : (v0 + BLOCK) * PACK].rearrange("p (v t) -> p v t", t=PACK),
                in_=acc[:].rearrange("p t v -> p v t"),
            )
            nc.scalar.copy(out=y[i][:, :, b * BLOCK : (b + 1) * BLOCK], in_=acc[:])

        def last_product(i, numbers):
            v0 = parts[i][0]
            acc = [bank(number, [P, 2, BLOCK], f"y_last{u}") for u, number in enumerate(numbers)]
            for k in range(STATS):
                for t in range(PACK):
                    one_pass(acc[t // 2][:, t % 2, :], i, 0, t, k, k == 0 and t % 2 == 0, k == STATS - 1 and t % 2 == 1)
            nc.scalar.copy(out=y[i][:, 0:2, :], in_=acc[0][:])
            nc.vector.tensor_copy(out=y[i][:, 2:4, :], in_=acc[1][:])
            nc.vector.tensor_copy(
                out=y_b[:, v0 * PACK : (v0 + BLOCK) * PACK].rearrange("p (n i t) -> p n t i", t=PACK, i=2),
                in_=y[i][:].rearrange("p t (n i) -> p n t i", i=2),
            )

        def store_result(i):
            v0, n = parts[i]
            nc.sync.dma_start(out=out_rows[:, :, v0 : v0 + n], in_=y[i][:])

        def quantize_result(i):
            v0, n = parts[i]
            quantize(y_codes, y_plane, v0, v0 + n, y_b[:, v0 * PACK : (v0 + n) * PACK])

        def store_words(v0, v1):
            nc.sync.dma_start(out=out_words[:, v0:v1], in_=y_codes[:, v0:v1].bitcast(I32))

        quantize(w_codes, w_plane, 0, 2 * T, w_b[:, 0 : 2 * PACK * T])
        quantize(w_codes, w_plane, 2 * T, STATS * T, w_b[:, 2 * PACK * T :])
        statistics(0, first_level(0))
        product(0, 0, 2)
        product(0, 1, 3)
        store_result(0)
        second_half = first_level(1)
        statistics(1, second_half)
        product(1, 0, 4)
        store_result(1)
        statistics(last_part, second_half)
        quantize_result(0)
        quantize_result(1)
        store_words(0, T - BLOCK)
        last_product(last_part, (5, 6))
        store_result(last_part)
        quantize_result(last_part)
        store_words(T - BLOCK, T)
        for q in range(QUADRANTS):
            queue = nc.sync if q < QUADRANTS // 2 else nc.scalar
            queue.dma_start(
                out=out_2[0, 4 * q : 4 * q + 4, :].bitcast(I32), in_=y_plane[32 * q : 32 * q + 4, :].bitcast(I32)
            )
